import numpy as np
import ml_dtypes


def mxq(x, axis, fmt="e4m3"):
    dtype, down = {"e4m3": (ml_dtypes.float8_e4m3fn, 7), "e5m2": (ml_dtypes.float8_e5m2, 14)}[fmt]
    v = np.moveaxis(np.asarray(x, np.float32).astype(ml_dtypes.bfloat16).astype(np.float64), axis, -1)
    blocks = v.reshape(v.shape[:-1] + (-1, 32))
    amax = np.abs(blocks).max(-1, keepdims=True)
    byte = np.maximum(np.where(amax > 0, np.frexp(amax)[1] - 1 + 127, 0) - down, 1)
    scale = np.exp2(byte - 127.0)
    codes = (blocks / scale).astype(np.float32).astype(dtype).astype(np.float64)
    return np.moveaxis((codes * scale).reshape(v.shape), -1, axis)


WIDE = False


def mx_kscale(k):
    if not WIDE:
        return np.ones(k)
    levels = np.array([30, -30])
    if k % 512:
        return np.exp2(np.random.permutation(np.resize(levels, k // 32))).repeat(32)
    a = np.empty((k // 512, 16))
    for p in range(k // 512):
        a[p, :8] = np.random.permutation(np.resize(levels, 8))
        for g in range(8):
            far = levels[np.abs(levels - a[p, g]) >= 10]
            a[p, g + 8] = far[np.random.randint(len(far))]
    return np.exp2(a.ravel()).repeat(32)


def f64(x):
    return np.asarray(x).astype(np.float64)


def striped(idx):
    return np.tile(np.asarray(idx).reshape(-1, 16).T, (8, 1)).astype(np.uint16)


def unstriped(offs):
    return offs[:16].T.reshape(-1).astype(np.int64)


E2M1 = np.array([0.0, 0.5, 1.0, 1.5, 2.0, 3.0, 4.0, 6.0, -0.0, -0.5, -1.0, -1.5, -2.0, -3.0, -4.0, -6.0])


def pack_weight(w, fmt):
    k, n = w.shape
    w = f64(np.asarray(w, np.float32).astype(ml_dtypes.bfloat16)).reshape(k // 32, 32, n)
    amax = np.abs(w).max(1)
    if fmt == "e4m3":
        byte = np.frexp(amax)[1] - 1 + 127 - 7
    else:
        mant, ex = np.frexp(amax / 6.0)
        byte = np.where(mant > 0.5, ex, ex - 1) + 127
    byte = np.clip(np.where(amax > 0, byte, 1), 1, 254)
    scaled = (w * np.exp2(127.0 - byte)[:, None, :]).reshape(k, n).astype(np.float32)
    by_word = np.ascontiguousarray(scaled.reshape(k // 512, 128, 4, n).transpose(0, 1, 3, 2))
    if fmt == "e4m3":
        words = by_word.astype(ml_dtypes.float8_e4m3fn).view(np.uint8)
    else:
        c = by_word.astype(ml_dtypes.float4_e2m1fn).view(np.uint8) & 0xF
        words = (c[..., 0::2] | (c[..., 1::2] << 4)).reshape(k // 512, 128, 2 * n)
    return np.ascontiguousarray(words), np.ascontiguousarray(byte.astype(np.uint8).reshape(k // 512, 16, n))


def unpack_weight(words, scales, fmt):
    g, _, n = scales.shape
    words = np.ascontiguousarray(words).reshape(g, 128, n, -1)
    if fmt == "e4m3":
        vals = words.view(ml_dtypes.float8_e4m3fn).astype(np.float64)
    else:
        nib = np.empty((g, 128, n, 4), np.uint8)
        nib[..., 0::2] = words & 0xF
        nib[..., 1::2] = words >> 4
        vals = E2M1[nib]
    vals = vals * np.repeat(np.exp2(scales.astype(np.float64) - 127.0), 8, axis=1)[..., None]
    return vals.transpose(0, 1, 3, 2).reshape(g * 512, n)


def sigmoid(v):
    return 1.0 / (1.0 + np.exp(-v))


K, T, Z, J, R, O, N, L, E = 512, 1024, 1024, 256, 512, 128, 256, 512, 512


def setup_inputs():
    n = np.random.standard_normal
    idx = np.random.permutation(T)[:J]
    idx2 = np.random.permutation(Z)[:J]
    idx3 = np.random.permutation(J)[:O]
    idx4 = np.random.permutation(J)[:O]
    idx5 = np.random.permutation(E)[:O]
    fk = mx_kscale(K)
    fr = mx_kscale(R)
    fl = mx_kscale(L)
    xtp = pack_weight(n((K, T)) / fk[:, None], "e2m1")
    xop = pack_weight(n((K, Z)) / fk[:, None], "e4m3")
    wp = pack_weight(n((K, R)) * 1 / np.sqrt(K) * fk[:, None] * fr, "e4m3")
    wbp = pack_weight(n((R, N)) * 1 / np.sqrt(R) / fr[:, None], "e2m1")
    sxp = pack_weight(n((L, O)) / fl[:, None], "e4m3")
    wsp = pack_weight(n((L, N)) * 1 / np.sqrt(L) * fl[:, None], "e4m3")
    return {
        "xt_words": xtp[0],
        "xt_scales": xtp[1],
        "xo_words": xop[0],
        "xo_scales": xop[1],
        "w_words": wp[0],
        "w_scales": wp[1],
        "wb_words": wbp[0],
        "wb_scales": wbp[1],
        "sx_words": sxp[0],
        "sx_scales": sxp[1],
        "ws_words": wsp[0],
        "ws_scales": wsp[1],
        "tz": (n((N, E))).astype(np.float32),
        "so": (np.random.uniform(0.6, 1.6, (N, 1))).astype(np.float32),
        "bo": (np.random.uniform(-1.0, 1.0, (N, 1))).astype(np.float32),
        "offs": striped(idx),
        "offs2": striped(idx2),
        "offs3": striped(idx3),
        "offs4": striped(idx4),
        "offs5": striped(idx5),
    }


def reference(xt_words, xt_scales, xo_words, xo_scales, w_words, w_scales, wb_words, wb_scales, sx_words, sx_scales, ws_words, ws_scales, tz, so, bo, offs, offs2, offs3, offs4, offs5):
    idx = unstriped(offs)
    idx2 = unstriped(offs2)
    idx3 = unstriped(offs3)
    idx4 = unstriped(offs4)
    idx5 = unstriped(offs5)
    xtu = unpack_weight(xt_words, xt_scales, "e2m1")
    xou = unpack_weight(xo_words, xo_scales, "e4m3")
    wu = unpack_weight(w_words, w_scales, "e4m3")
    wbu = unpack_weight(wb_words, wb_scales, "e2m1")
    sxu = unpack_weight(sx_words, sx_scales, "e4m3")
    wsu = unpack_weight(ws_words, ws_scales, "e4m3")
    xtidxg = xtu[:, idx]
    a = wu.T @ xtidxg
    xoidx2g = xou[:, idx2]
    b = wu.T @ xoidx2g
    hid = np.abs(a[:, idx3] - b[:, idx4])
    hidq = mxq(hid, 0, "e5m2")
    p = wbu.T @ hidq + wsu.T @ sxu
    y = p * sigmoid(f64(tz)[:, idx5] * f64(so) + f64(bo))
    return y

@@ -1,0 +1,159 @@
+from contextlib import ExitStack
+
+import concourse.mybir as mybir
+
+K, T, Z, J, R, O, N, L, E = 512, 1024, 1024, 256, 512, 128, 256, 512, 512
+FLOPS = 2 * (2 * K * R * J) + 2 * R * N * O + 2 * L * N * O
+
+F32 = mybir.dt.float32
+BF16 = mybir.dt.bfloat16
+I32 = mybir.dt.int32
+U32 = mybir.dt.uint32
+U16 = mybir.dt.uint16
+U8 = mybir.dt.uint8
+E4M3X4 = mybir.dt.float8_e4m3fn_x4
+E5M2X4 = mybir.dt.float8_e5m2_x4
+E2M1X4 = mybir.dt.float4_e2m1fn_x4
+ACT = mybir.ActivationFunctionType
+ALU = mybir.AluOpType
+
+P = 128
+PACK = 4
+HALVES = N // P
+
+
+def tile_list_oneforboth_looked_skip_finalgate_kernel(
+    tc, xt_words, xt_scales, xo_words, xo_scales, w_words, w_scales, wb_words, wb_scales,
+    sx_words, sx_scales, ws_words, ws_scales, tz, so, bo, offs, offs2, offs3, offs4, offs5, out,
+):
+    nc = tc.nc
+    with ExitStack() as ctx:
+        sb = ctx.enter_context(tc.tile_pool(name="sb", bufs=1))
+        ps = ctx.enter_context(tc.psum_pool(name="ps", bufs=1))
+
+        def load_list(src, name):
+            t = sb.tile(list(src.shape), U16, name=name)
+            nc.sync.dma_start(t[:], src)
+            return t
+
+        def load_words(src, dtype, width, name, queue):
+            t = sb.tile([P, width], dtype, name=name, align_bytes=64)
+            queue.dma_start(out=t[:].bitcast(I32), in_=src.bitcast(I32))
+            return t
+
+        def zeroed_plane(src, name, engine):
+            t = sb.tile([P, src.shape[2]], U8, name=name, align_bytes=64)
+            engine.memset(t[:].bitcast(I32), 0)
+            return t
+
+        def load_scales(plane, src, queue):
+            for q in range(4):
+                queue.dma_start(out=plane[32 * q:32 * q + 4, :].bitcast(I32), in_=src[0, 4 * q:4 * q + 4, :].bitcast(I32))
+
+
+        def e4m3_words(src):
+            return src[0].rearrange("p n t -> p (n t)")
+
+        xt_sc = zeroed_plane(xt_scales, "xt_sc", nc.vector)
+        w_sc_raw = zeroed_plane(w_scales, "w_sc_raw", nc.vector)
+        xo_sc = zeroed_plane(xo_scales, "xo_sc", nc.gpsimd)
+        wb_sc = zeroed_plane(wb_scales, "wb_sc", nc.gpsimd)
+        ws_sc = zeroed_plane(ws_scales, "ws_sc", nc.vector)
+        sx_sc = zeroed_plane(sx_scales, "sx_sc", nc.vector)
+        xt_w = load_words(xt_words[0], U16, T, "xt_w", nc.scalar)
+        w_raw = load_words(e4m3_words(w_words), I32, R, "w_raw", nc.scalar)
+        xo_w = load_words(e4m3_words(xo_words), U32, Z, "xo_w", nc.scalar)
+        list1 = load_list(offs, "list1")
+        load_scales(xt_sc, xt_scales, nc.sync)
+        load_scales(w_sc_raw, w_scales, nc.sync)
+        load_scales(xo_sc, xo_scales, nc.gpsimd)
+        load_scales(wb_sc, wb_scales, nc.gpsimd)
+        list2 = load_list(offs2, "list2")
+        list3 = load_list(offs3, "list3")
+        list4 = load_list(offs4, "list4")
+        list5 = load_list(offs5, "list5")
+        slope = sb.tile([P, HALVES], F32, name="slope")
+        offset = sb.tile([P, HALVES], F32, name="offset")
+        with nc.allow_non_contiguous_dma(reason="one value a partition"):
+            nc.sync.dma_start(out=slope[:], in_=so.rearrange("(h p) one -> p (h one)", p=P))
+            nc.sync.dma_start(out=offset[:], in_=bo.rearrange("(h p) one -> p (h one)", p=P))
+        tz_rows = []
+        for h in range(HALVES):
+            rows = sb.tile([P, E], F32, name="tz_rows%d" % h)
+            nc.sync.dma_start(out=rows[:], in_=tz[h * P:(h + 1) * P, :])
+            tz_rows.append(rows)
+        ws_w = load_words(e4m3_words(ws_words), U32, N, "ws_w", nc.sync)
+        sx_w = load_words(e4m3_words(sx_words), U32, O, "sx_w", nc.sync)
+        wb_w = load_words(wb_words[0], U16, N, "wb_w", nc.sync)
+        load_scales(ws_sc, ws_scales, nc.sync)
+        load_scales(sx_sc, sx_scales, nc.sync)
+
+        xt_g = sb.tile([P, J], U16, name="xt_g", align_bytes=64)
+        xt_gs = sb.tile([P, J], U8, name="xt_gs", align_bytes=64)
+        xo_g = sb.tile([P, J], U32, name="xo_g", align_bytes=64)
+        xo_gs = sb.tile([P, J], U8, name="xo_gs", align_bytes=64)
+        w_w = sb.tile([P, R], I32, name="w_w", align_bytes=64)
+        w_sc = sb.tile([P, R], U8, name="w_sc", align_bytes=64)
+        nc.vector.tensor_copy(out=xt_gs[:], in_=xt_sc[:].indirect(list1[:]))
+        nc.vector.tensor_copy(out=xt_g[:], in_=xt_w[:].indirect(list1[:]))
+        for dealt, raw in ((w_w, w_raw), (w_sc, w_sc_raw)):
+            nc.vector.tensor_copy(
+                out=dealt[:].rearrange("p (t c i) -> p c t i", t=PACK, i=PACK),
+                in_=raw[:].rearrange("p (c i t) -> p c t i", t=PACK, i=PACK),
+            )
+        nc.vector.tensor_copy(out=xo_g[:], in_=xo_w[:].indirect(list2[:]))
+        nc.vector.tensor_copy(out=xo_gs[:], in_=xo_sc[:].indirect(list2[:]))
+
+        def first_stage(dst, t, moving, moving_scale):
+            cols = slice(t * P, (t + 1) * P)
+            nc.tensor.matmul_mx(out=dst, lhsT=w_w[:, cols].bitcast(E4M3X4), lhsT_scale=w_sc[:, cols],
+                                rhs=moving, rhs_scale=moving_scale, start=True, stop=True)
+
+        a_ps = [ps.tile([P, 2 * J], F32, name="a_ps%d" % u) for u in range(PACK // 2)]
+        b_ps = [ps.tile([P, J], F32, name="b_ps%d" % t) for t in range(PACK)]
+        p_ps = [ps.tile([P, O], F32, name="p_ps%d" % h) for h in range(HALVES)]
+        for t in range(PACK):
+            first_stage(a_ps[t // 2][:, (t % 2) * J:(t % 2 + 1) * J], t, xt_g[:].bitcast(E2M1X4), xt_gs[:])
+        for t in range(PACK):
+            first_stage(b_ps[t][:], t, xo_g[:].bitcast(E4M3X4), xo_gs[:])
+        for h in range(HALVES):
+            cols = slice(h * P, (h + 1) * P)
+            nc.tensor.matmul_mx(out=p_ps[h][:], lhsT=ws_w[:, cols].bitcast(E4M3X4), lhsT_scale=ws_sc[:, cols],
+                                rhs=sx_w[:].bitcast(E4M3X4), rhs_scale=sx_sc[:], start=True, stop=False)
+
+        a_pick = []
+        for u in range(PACK // 2):
+            a_sb = sb.tile([P, 2 * J], F32, name="a_sb%d" % u)
+            nc.scalar.activation(out=a_sb[:], in_=a_ps[u][:], func=ACT.Copy)
+            for v in range(2):
+                pick = sb.tile([P, O], F32, name="a_pick%d" % (2 * u + v))
+                nc.scalar.activation(out=pick[:], in_=a_sb[:, v * J:(v + 1) * J].indirect(list3[:]), func=ACT.Copy)
+                a_pick.append(pick)
+
+        diff = [sb.tile([P, 2, O], F32, name="diff%d" % u) for u in range(PACK // 2)]
+        hid = sb.tile([P, O, PACK], BF16, name="hid", align_bytes=64)
+        for t in range(PACK):
+            b_sb = sb.tile([P, J], F32, name="b_sb%d" % t)
+            if t < PACK - 1:
+                nc.vector.tensor_copy(out=b_sb[:], in_=b_ps[t][:])
+            else:
+                nc.scalar.activation(out=b_sb[:], in_=b_ps[t][:], func=ACT.Copy)
+            nc.vector.tensor_tensor(out=diff[t // 2][:, t % 2, :], in0=b_sb[:].indirect(list4[:]), in1=a_pick[t][:], op=ALU.subtract)
+            if t % 2 == 1:
+                nc.scalar.activation(out=hid[:, :, t - 1:t + 1], in_=diff[t // 2][:].rearrange("p v o -> p o v"), func=ACT.Abs)
+
+        hid_w = sb.tile([P, O], U32, name="hid_w", align_bytes=64)
+        hid_sc = sb.tile([P, O], U8, name="hid_sc", align_bytes=64)
+        nc.vector.quantize_mx(out=hid_w[:].bitcast(E5M2X4), scales=hid_sc[:], in_=hid[:].rearrange("p o t -> p (o t)"))
+
+        for h in range(HALVES):
+            cols = slice(h * P, (h + 1) * P)
+            nc.tensor.matmul_mx(out=p_ps[h][:], lhsT=wb_w[:, cols].bitcast(E2M1X4), lhsT_scale=wb_sc[:, cols],
+                                rhs=hid_w[:].bitcast(E5M2X4), rhs_scale=hid_sc[:], start=False, stop=True)
+        for h in range(HALVES):
+            gate = sb.tile([P, O], F32, name="gate%d" % h)
+            nc.scalar.activation(out=gate[:], in_=tz_rows[h][:].indirect(list5[:]), func=ACT.Sigmoid,
+                                 bias=offset[:, h:h + 1], scale=slope[:, h:h + 1])
+            res = sb.tile([P, O], F32, name="res%d" % h)
+            nc.vector.tensor_tensor(out=res[:], in0=p_ps[h][:], in1=gate[:], op=ALU.mult)
+            nc.sync.dma_start(out=out[h * P:(h + 1) * P, :], in_=res[:])

@@ -29,6 +29,7 @@ def tile_list_oneforboth_looked_skip_finalgate_kernel(
     nc = tc.nc
     with ExitStack() as ctx:
         sb = ctx.enter_context(tc.tile_pool(name="sb", bufs=1))
+        reuse = ctx.enter_context(tc.tile_pool(name="reuse", bufs=1))
         ps = ctx.enter_context(tc.psum_pool(name="ps", bufs=1))
 
         def load_list(src, name):
@@ -41,42 +42,43 @@ def tile_list_oneforboth_looked_skip_finalgate_kernel(
             queue.dma_start(out=t[:].bitcast(I32), in_=src.bitcast(I32))
             return t
 
-        def zeroed_plane(src, name, engine):
-            t = sb.tile([P, src.shape[2]], U8, name=name, align_bytes=64)
+        def zeroed_plane(width, name, engine):
+            t = sb.tile([P, width], U8, name=name, align_bytes=64)
             engine.memset(t[:].bitcast(I32), 0)
             return t
 
-        def load_scales(plane, src, queue):
-            for q in range(4):
-                queue.dma_start(out=plane[32 * q:32 * q + 4, :].bitcast(I32), in_=src[0, 4 * q:4 * q + 4, :].bitcast(I32))
+        def load_scales(plane, src, queues):
+            for q, queue in enumerate(queues):
+                rows = src[0, 4 * q:4 * q + 4, :].bitcast(I32)
+                queue.dma_start(out=plane[32 * q:32 * q + 32, :].bitcast(I32),
+                                in_=rows.unsqueeze(0).to_broadcast([8, 4, rows.shape[1]]))
 
 
         def e4m3_words(src):
             return src[0].rearrange("p n t -> p (n t)")
 
-        xt_sc = zeroed_plane(xt_scales, "xt_sc", nc.vector)
-        w_sc_raw = zeroed_plane(w_scales, "w_sc_raw", nc.vector)
-        xo_sc = zeroed_plane(xo_scales, "xo_sc", nc.gpsimd)
-        wb_sc = zeroed_plane(wb_scales, "wb_sc", nc.gpsimd)
-        ws_sc = zeroed_plane(ws_scales, "ws_sc", nc.vector)
-        sx_sc = zeroed_plane(sx_scales, "sx_sc", nc.vector)
+        xt_sc = sb.tile([P, T], U8, name="xt_sc", align_bytes=64)
+        w_sc_raw = reuse.tile([P, R], U8, name="w_sc_raw", align_bytes=64, offset=0)
+        xo_sc = sb.tile([P, Z], U8, name="xo_sc", align_bytes=64)
+        late_sc = zeroed_plane(N + O + N, "late_sc", nc.vector)
+        warm = sb.tile([P, 1], F32, name="warm")
+        warm_out = sb.tile([P, 1], F32, name="warm_out")
+        nc.vector.memset(warm[:], 0.0)
         xt_w = load_words(xt_words[0], U16, T, "xt_w", nc.scalar)
         w_raw = load_words(e4m3_words(w_words), I32, R, "w_raw", nc.scalar)
-        xo_w = load_words(e4m3_words(xo_words), U32, Z, "xo_w", nc.scalar)
+        nc.scalar.activation(out=warm_out[:], in_=warm[:], func=ACT.Sigmoid)
         list1 = load_list(offs, "list1")
-        load_scales(xt_sc, xt_scales, nc.sync)
-        load_scales(w_sc_raw, w_scales, nc.sync)
-        load_scales(xo_sc, xo_scales, nc.gpsimd)
-        load_scales(wb_sc, wb_scales, nc.gpsimd)
+        load_scales(xt_sc, xt_scales, [nc.sync] * 4)
+        load_scales(w_sc_raw, w_scales, [nc.sync] * 2 + [nc.gpsimd] * 2)
+        xo_w = load_words(e4m3_words(xo_words), U32, Z, "xo_w", nc.sync)
         list2 = load_list(offs2, "list2")
+        load_scales(xo_sc, xo_scales, [nc.sync] * 4)
         list3 = load_list(offs3, "list3")
         list4 = load_list(offs4, "list4")
-        list5 = load_list(offs5, "list5")
-        slope = sb.tile([P, HALVES], F32, name="slope")
-        offset = sb.tile([P, HALVES], F32, name="offset")
-        with nc.allow_non_contiguous_dma(reason="one value a partition"):
-            nc.sync.dma_start(out=slope[:], in_=so.rearrange("(h p) one -> p (h one)", p=P))
-            nc.sync.dma_start(out=offset[:], in_=bo.rearrange("(h p) one -> p (h one)", p=P))
+        late_rows = sb.tile([16, (N + O + N) // 4], I32, name="late_rows")
+        ws_cols, sx_cols, wb_cols = slice(0, N), slice(N, N + O), slice(N + O, N + O + N)
+        for src, cols in ((ws_scales, ws_cols), (sx_scales, sx_cols), (wb_scales, wb_cols)):
+            nc.sync.dma_start(out=late_rows[:, cols.start // 4:cols.stop // 4], in_=src[0].bitcast(I32))
         tz_rows = []
         for h in range(HALVES):
             rows = sb.tile([P, E], F32, name="tz_rows%d" % h)
@@ -85,13 +87,20 @@ def tile_list_oneforboth_looked_skip_finalgate_kernel(
         ws_w = load_words(e4m3_words(ws_words), U32, N, "ws_w", nc.sync)
         sx_w = load_words(e4m3_words(sx_words), U32, O, "sx_w", nc.sync)
         wb_w = load_words(wb_words[0], U16, N, "wb_w", nc.sync)
-        load_scales(ws_sc, ws_scales, nc.sync)
-        load_scales(sx_sc, sx_scales, nc.sync)
+        list5 = load_list(offs5, "list5")
+        slope = sb.tile([P, HALVES], F32, name="slope")
+        offset = sb.tile([P, HALVES], F32, name="offset")
+        with nc.allow_non_contiguous_dma(reason="one value a partition"):
+            nc.sync.dma_start(out=slope[:], in_=so.rearrange("(h p) one -> p (h one)", p=P))
+            nc.sync.dma_start(out=offset[:], in_=bo.rearrange("(h p) one -> p (h one)", p=P))
+        for q in range(4):
+            nc.sync.dma_start(out=late_sc[32 * q:32 * q + 4, :].bitcast(I32), in_=late_rows[4 * q:4 * q + 4, :])
+        ws_sc, sx_sc, wb_sc = late_sc[:, ws_cols], late_sc[:, sx_cols], late_sc[:, wb_cols]
 
         xt_g = sb.tile([P, J], U16, name="xt_g", align_bytes=64)
         xt_gs = sb.tile([P, J], U8, name="xt_gs", align_bytes=64)
-        xo_g = sb.tile([P, J], U32, name="xo_g", align_bytes=64)
-        xo_gs = sb.tile([P, J], U8, name="xo_gs", align_bytes=64)
+        xo_g = reuse.tile([P, J], U32, name="xo_g", align_bytes=64, offset=J)
+        xo_gs = reuse.tile([P, J], U8, name="xo_gs", align_bytes=64, offset=0)
         w_w = sb.tile([P, R], I32, name="w_w", align_bytes=64)
         w_sc = sb.tile([P, R], U8, name="w_sc", align_bytes=64)
         nc.vector.tensor_copy(out=xt_gs[:], in_=xt_sc[:].indirect(list1[:]))
@@ -109,38 +118,47 @@ def tile_list_oneforboth_looked_skip_finalgate_kernel(
             nc.tensor.matmul_mx(out=dst, lhsT=w_w[:, cols].bitcast(E4M3X4), lhsT_scale=w_sc[:, cols],
                                 rhs=moving, rhs_scale=moving_scale, start=True, stop=True)
 
-        a_ps = [ps.tile([P, 2 * J], F32, name="a_ps%d" % u) for u in range(PACK // 2)]
+        a_ps = [ps.tile([P, J], F32, name="a_ps%d" % t, tag="bank%d" % t) for t in range(PACK)]
         b_ps = [ps.tile([P, J], F32, name="b_ps%d" % t) for t in range(PACK)]
-        p_ps = [ps.tile([P, O], F32, name="p_ps%d" % h) for h in range(HALVES)]
         for t in range(PACK):
-            first_stage(a_ps[t // 2][:, (t % 2) * J:(t % 2 + 1) * J], t, xt_g[:].bitcast(E2M1X4), xt_gs[:])
+            first_stage(a_ps[t][:], t, xt_g[:].bitcast(E2M1X4), xt_gs[:])
         for t in range(PACK):
             first_stage(b_ps[t][:], t, xo_g[:].bitcast(E4M3X4), xo_gs[:])
+
+        a_sb = [sb.tile([P, J], F32, name="a_sb%d" % t) for t in range(PACK)]
+        b_sb = [sb.tile([P, J], F32, name="b_sb%d" % t) for t in range(PACK)]
+        a_pick = [sb.tile([P, O], F32, name="a_pick%d" % t) for t in range(PACK)]
+        diff = [sb.tile([P, 2, O], F32, name="diff%d" % u, tag="pair%d" % u) for u in range(PACK // 2)]
+        hid = sb.tile([P, O, PACK], BF16, name="hid", align_bytes=64)
+
+        def scalar_evict(dst, src):
+            nc.scalar.activation(out=dst[:], in_=src[:], func=ACT.Copy)
+
+        def pick_a(t):
+            nc.scalar.activation(out=a_pick[t][:], in_=a_sb[t][:].indirect(list3[:]), func=ACT.Copy)
+
+        def subtract(t):
+            nc.vector.tensor_tensor(out=diff[t // 2][:, t % 2, :], in0=b_sb[t][:].indirect(list4[:]), in1=a_pick[t][:], op=ALU.subtract)
+
+        scalar_evict(a_sb[0], a_ps[0])
+        for t in range(1, PACK):
+            scalar_evict(a_sb[t], a_ps[t])
+            pick_a(t - 1)
+        scalar_evict(b_sb[2], b_ps[2])
+        pick_a(3)
+        scalar_evict(b_sb[3], b_ps[3])
+        for t in range(2):
+            nc.vector.tensor_copy(out=b_sb[t][:], in_=b_ps[t][:])
+        for t in range(PACK):
+            subtract(t)
+        for u in range(PACK // 2):
+            nc.scalar.activation(out=hid[:, :, 2 * u:2 * u + 2], in_=diff[u][:].rearrange("p v o -> p o v"), func=ACT.Abs)
+
+        p_ps = ps.tile([P, HALVES * O], F32, name="p_ps", tag="bank0")
         for h in range(HALVES):
             cols = slice(h * P, (h + 1) * P)
-            nc.tensor.matmul_mx(out=p_ps[h][:], lhsT=ws_w[:, cols].bitcast(E4M3X4), lhsT_scale=ws_sc[:, cols],
-                                rhs=sx_w[:].bitcast(E4M3X4), rhs_scale=sx_sc[:], start=True, stop=False)
-
-        a_pick = []
-        for u in range(PACK // 2):
-            a_sb = sb.tile([P, 2 * J], F32, name="a_sb%d" % u)
-            nc.scalar.activation(out=a_sb[:], in_=a_ps[u][:], func=ACT.Copy)
-            for v in range(2):
-                pick = sb.tile([P, O], F32, name="a_pick%d" % (2 * u + v))
-                nc.scalar.activation(out=pick[:], in_=a_sb[:, v * J:(v + 1) * J].indirect(list3[:]), func=ACT.Copy)
-                a_pick.append(pick)
-
-        diff = [sb.tile([P, 2, O], F32, name="diff%d" % u) for u in range(PACK // 2)]
-        hid = sb.tile([P, O, PACK], BF16, name="hid", align_bytes=64)
-        for t in range(PACK):
-            b_sb = sb.tile([P, J], F32, name="b_sb%d" % t)
-            if t < PACK - 1:
-                nc.vector.tensor_copy(out=b_sb[:], in_=b_ps[t][:])
-            else:
-                nc.scalar.activation(out=b_sb[:], in_=b_ps[t][:], func=ACT.Copy)
-            nc.vector.tensor_tensor(out=diff[t // 2][:, t % 2, :], in0=b_sb[:].indirect(list4[:]), in1=a_pick[t][:], op=ALU.subtract)
-            if t % 2 == 1:
-                nc.scalar.activation(out=hid[:, :, t - 1:t + 1], in_=diff[t // 2][:].rearrange("p v o -> p o v"), func=ACT.Abs)
+            nc.tensor.matmul_mx(out=p_ps[:, h * O:(h + 1) * O], lhsT=ws_w[:, cols].bitcast(E4M3X4), lhsT_scale=ws_sc[:, cols],
+                                rhs=sx_w[:].bitcast(E4M3X4), rhs_scale=sx_sc, start=(h == 0), stop=False)
 
         hid_w = sb.tile([P, O], U32, name="hid_w", align_bytes=64)
         hid_sc = sb.tile([P, O], U8, name="hid_sc", align_bytes=64)
@@ -148,12 +166,12 @@ def tile_list_oneforboth_looked_skip_finalgate_kernel(
 
         for h in range(HALVES):
             cols = slice(h * P, (h + 1) * P)
-            nc.tensor.matmul_mx(out=p_ps[h][:], lhsT=wb_w[:, cols].bitcast(E2M1X4), lhsT_scale=wb_sc[:, cols],
-                                rhs=hid_w[:].bitcast(E5M2X4), rhs_scale=hid_sc[:], start=False, stop=True)
+            nc.tensor.matmul_mx(out=p_ps[:, h * O:(h + 1) * O], lhsT=wb_w[:, cols].bitcast(E2M1X4), lhsT_scale=wb_sc[:, cols],
+                                rhs=hid_w[:].bitcast(E5M2X4), rhs_scale=hid_sc[:], start=False, stop=(h == HALVES - 1))
+        gate = sb.tile([P, HALVES, O], F32, name="gate", tag="pair1")
         for h in range(HALVES):
-            gate = sb.tile([P, O], F32, name="gate%d" % h)
-            nc.scalar.activation(out=gate[:], in_=tz_rows[h][:].indirect(list5[:]), func=ACT.Sigmoid,
+            nc.scalar.activation(out=gate[:, h, :], in_=tz_rows[h][:].indirect(list5[:]), func=ACT.Sigmoid,
                                  bias=offset[:, h:h + 1], scale=slope[:, h:h + 1])
-            res = sb.tile([P, O], F32, name="res%d" % h)
-            nc.vector.tensor_tensor(out=res[:], in0=p_ps[h][:], in1=gate[:], op=ALU.mult)
-            nc.sync.dma_start(out=out[h * P:(h + 1) * P, :], in_=res[:])
+        res = sb.tile([P, HALVES, O], F32, name="res")
+        nc.vector.tensor_tensor(out=res[:].rearrange("p h o -> p (h o)"), in0=p_ps[:], in1=gate[:].rearrange("p h o -> p (h o)"), op=ALU.mult)
+        nc.sync.dma_start(out=out.rearrange("(h p) o -> p h o", p=P), in_=res[:])

from contextlib import ExitStack

import concourse.mybir as mybir

K, T, Z, J, R, O, N, L, E = 512, 1024, 1024, 256, 512, 128, 256, 512, 512
FLOPS = 2 * (2 * K * R * J) + 2 * R * N * O + 2 * L * N * O

F32 = mybir.dt.float32
BF16 = mybir.dt.bfloat16
I32 = mybir.dt.int32
U32 = mybir.dt.uint32
U16 = mybir.dt.uint16
U8 = mybir.dt.uint8
E4M3X4 = mybir.dt.float8_e4m3fn_x4
E5M2X4 = mybir.dt.float8_e5m2_x4
E2M1X4 = mybir.dt.float4_e2m1fn_x4
ACT = mybir.ActivationFunctionType
ALU = mybir.AluOpType

P = 128
PACK = 4
HALVES = N // P


def tile_list_oneforboth_looked_skip_finalgate_kernel(
    tc, xt_words, xt_scales, xo_words, xo_scales, w_words, w_scales, wb_words, wb_scales,
    sx_words, sx_scales, ws_words, ws_scales, tz, so, bo, offs, offs2, offs3, offs4, offs5, out,
):
    nc = tc.nc
    with ExitStack() as ctx:
        sb = ctx.enter_context(tc.tile_pool(name="sb", bufs=1))
        reuse = ctx.enter_context(tc.tile_pool(name="reuse", bufs=1))
        ps = ctx.enter_context(tc.psum_pool(name="ps", bufs=1))

        def load_list(src, name):
            t = sb.tile(list(src.shape), U16, name=name)
            nc.sync.dma_start(t[:], src)
            return t

        def load_words(src, dtype, width, name, queue):
            t = sb.tile([P, width], dtype, name=name, align_bytes=64)
            queue.dma_start(out=t[:].bitcast(I32), in_=src.bitcast(I32))
            return t

        def zeroed_plane(width, name, engine):
            t = sb.tile([P, width], U8, name=name, align_bytes=64)
            engine.memset(t[:].bitcast(I32), 0)
            return t

        def load_scales(plane, src, queues):
            for q, queue in enumerate(queues):
                rows = src[0, 4 * q:4 * q + 4, :].bitcast(I32)
                queue.dma_start(out=plane[32 * q:32 * q + 32, :].bitcast(I32),
                                in_=rows.unsqueeze(0).to_broadcast([8, 4, rows.shape[1]]))


        def e4m3_words(src):
            return src[0].rearrange("p n t -> p (n t)")

        xt_sc = sb.tile([P, T], U8, name="xt_sc", align_bytes=64)
        w_sc_raw = reuse.tile([P, R], U8, name="w_sc_raw", align_bytes=64, offset=0)
        xo_sc = sb.tile([P, Z], U8, name="xo_sc", align_bytes=64)
        late_sc = zeroed_plane(N + O + N, "late_sc", nc.vector)
        warm = sb.tile([P, 1], F32, name="warm")
        warm_out = sb.tile([P, 1], F32, name="warm_out")
        nc.vector.memset(warm[:], 0.0)
        xt_w = load_words(xt_words[0], U16, T, "xt_w", nc.scalar)
        w_raw = load_words(e4m3_words(w_words), I32, R, "w_raw", nc.scalar)
        nc.scalar.activation(out=warm_out[:], in_=warm[:], func=ACT.Sigmoid)
        list1 = load_list(offs, "list1")
        load_scales(xt_sc, xt_scales, [nc.sync] * 4)
        load_scales(w_sc_raw, w_scales, [nc.sync] * 2 + [nc.gpsimd] * 2)
        xo_w = load_words(e4m3_words(xo_words), U32, Z, "xo_w", nc.sync)
        list2 = load_list(offs2, "list2")
        load_scales(xo_sc, xo_scales, [nc.sync] * 4)
        list3 = load_list(offs3, "list3")
        list4 = load_list(offs4, "list4")
        late_rows = sb.tile([16, (N + O + N) // 4], I32, name="late_rows")
        ws_cols, sx_cols, wb_cols = slice(0, N), slice(N, N + O), slice(N + O, N + O + N)
        for src, cols in ((ws_scales, ws_cols), (sx_scales, sx_cols), (wb_scales, wb_cols)):
            nc.sync.dma_start(out=late_rows[:, cols.start // 4:cols.stop // 4], in_=src[0].bitcast(I32))
        tz_rows = []
        for h in range(HALVES):
            rows = sb.tile([P, E], F32, name="tz_rows%d" % h)
            nc.sync.dma_start(out=rows[:], in_=tz[h * P:(h + 1) * P, :])
            tz_rows.append(rows)
        ws_w = load_words(e4m3_words(ws_words), U32, N, "ws_w", nc.sync)
        sx_w = load_words(e4m3_words(sx_words), U32, O, "sx_w", nc.sync)
        wb_w = load_words(wb_words[0], U16, N, "wb_w", nc.sync)
        list5 = load_list(offs5, "list5")
        slope = sb.tile([P, HALVES], F32, name="slope")
        offset = sb.tile([P, HALVES], F32, name="offset")
        with nc.allow_non_contiguous_dma(reason="one value a partition"):
            nc.sync.dma_start(out=slope[:], in_=so.rearrange("(h p) one -> p (h one)", p=P))
            nc.sync.dma_start(out=offset[:], in_=bo.rearrange("(h p) one -> p (h one)", p=P))
        for q in range(4):
            nc.sync.dma_start(out=late_sc[32 * q:32 * q + 4, :].bitcast(I32), in_=late_rows[4 * q:4 * q + 4, :])
        ws_sc, sx_sc, wb_sc = late_sc[:, ws_cols], late_sc[:, sx_cols], late_sc[:, wb_cols]

        xt_g = sb.tile([P, J], U16, name="xt_g", align_bytes=64)
        xt_gs = sb.tile([P, J], U8, name="xt_gs", align_bytes=64)
        xo_g = reuse.tile([P, J], U32, name="xo_g", align_bytes=64, offset=J)
        xo_gs = reuse.tile([P, J], U8, name="xo_gs", align_bytes=64, offset=0)
        w_w = sb.tile([P, R], I32, name="w_w", align_bytes=64)
        w_sc = sb.tile([P, R], U8, name="w_sc", align_bytes=64)
        nc.vector.tensor_copy(out=xt_gs[:], in_=xt_sc[:].indirect(list1[:]))
        nc.vector.tensor_copy(out=xt_g[:], in_=xt_w[:].indirect(list1[:]))
        for dealt, raw in ((w_w, w_raw), (w_sc, w_sc_raw)):
            nc.vector.tensor_copy(
                out=dealt[:].rearrange("p (t c i) -> p c t i", t=PACK, i=PACK),
                in_=raw[:].rearrange("p (c i t) -> p c t i", t=PACK, i=PACK),
            )
        nc.vector.tensor_copy(out=xo_g[:], in_=xo_w[:].indirect(list2[:]))
        nc.vector.tensor_copy(out=xo_gs[:], in_=xo_sc[:].indirect(list2[:]))

        def first_stage(dst, t, moving, moving_scale):
            cols = slice(t * P, (t + 1) * P)
            nc.tensor.matmul_mx(out=dst, lhsT=w_w[:, cols].bitcast(E4M3X4), lhsT_scale=w_sc[:, cols],
                                rhs=moving, rhs_scale=moving_scale, start=True, stop=True)

        a_ps = [ps.tile([P, J], F32, name="a_ps%d" % t, tag="bank%d" % t) for t in range(PACK)]
        b_ps = [ps.tile([P, J], F32, name="b_ps%d" % t) for t in range(PACK)]
        for t in range(PACK):
            first_stage(a_ps[t][:], t, xt_g[:].bitcast(E2M1X4), xt_gs[:])
        for t in range(PACK):
            first_stage(b_ps[t][:], t, xo_g[:].bitcast(E4M3X4), xo_gs[:])

        a_sb = [sb.tile([P, J], F32, name="a_sb%d" % t) for t in range(PACK)]
        b_sb = [sb.tile([P, J], F32, name="b_sb%d" % t) for t in range(PACK)]
        a_pick = [sb.tile([P, O], F32, name="a_pick%d" % t) for t in range(PACK)]
        diff = [sb.tile([P, 2, O], F32, name="diff%d" % u, tag="pair%d" % u) for u in range(PACK // 2)]
        hid = sb.tile([P, O, PACK], BF16, name="hid", align_bytes=64)

        def scalar_evict(dst, src):
            nc.scalar.activation(out=dst[:], in_=src[:], func=ACT.Copy)

        def pick_a(t):
            nc.scalar.activation(out=a_pick[t][:], in_=a_sb[t][:].indirect(list3[:]), func=ACT.Copy)

        def subtract(t):
            nc.vector.tensor_tensor(out=diff[t // 2][:, t % 2, :], in0=b_sb[t][:].indirect(list4[:]), in1=a_pick[t][:], op=ALU.subtract)

        scalar_evict(a_sb[0], a_ps[0])
        for t in range(1, PACK):
            scalar_evict(a_sb[t], a_ps[t])
            pick_a(t - 1)
        scalar_evict(b_sb[2], b_ps[2])
        pick_a(3)
        scalar_evict(b_sb[3], b_ps[3])
        for t in range(2):
            nc.vector.tensor_copy(out=b_sb[t][:], in_=b_ps[t][:])
        for t in range(PACK):
            subtract(t)
        for u in range(PACK // 2):
            nc.scalar.activation(out=hid[:, :, 2 * u:2 * u + 2], in_=diff[u][:].rearrange("p v o -> p o v"), func=ACT.Abs)

        p_ps = ps.tile([P, HALVES * O], F32, name="p_ps", tag="bank0")
        for h in range(HALVES):
            cols = slice(h * P, (h + 1) * P)
            nc.tensor.matmul_mx(out=p_ps[:, h * O:(h + 1) * O], lhsT=ws_w[:, cols].bitcast(E4M3X4), lhsT_scale=ws_sc[:, cols],
                                rhs=sx_w[:].bitcast(E4M3X4), rhs_scale=sx_sc, start=(h == 0), stop=False)

        hid_w = sb.tile([P, O], U32, name="hid_w", align_bytes=64)
        hid_sc = sb.tile([P, O], U8, name="hid_sc", align_bytes=64)
        nc.vector.quantize_mx(out=hid_w[:].bitcast(E5M2X4), scales=hid_sc[:], in_=hid[:].rearrange("p o t -> p (o t)"))

        for h in range(HALVES):
            cols = slice(h * P, (h + 1) * P)
            nc.tensor.matmul_mx(out=p_ps[:, h * O:(h + 1) * O], lhsT=wb_w[:, cols].bitcast(E2M1X4), lhsT_scale=wb_sc[:, cols],
                                rhs=hid_w[:].bitcast(E5M2X4), rhs_scale=hid_sc[:], start=False, stop=(h == HALVES - 1))
        gate = sb.tile([P, HALVES, O], F32, name="gate", tag="pair1")
        for h in range(HALVES):
            nc.scalar.activation(out=gate[:, h, :], in_=tz_rows[h][:].indirect(list5[:]), func=ACT.Sigmoid,
                                 bias=offset[:, h:h + 1], scale=slope[:, h:h + 1])
        res = sb.tile([P, HALVES, O], F32, name="res")
        nc.vector.tensor_tensor(out=res[:].rearrange("p h o -> p (h o)"), in0=p_ps[:], in1=gate[:].rearrange("p h o -> p (h o)"), op=ALU.mult)
        nc.sync.dma_start(out=out.rearrange("(h p) o -> p h o", p=P), in_=res[:])
